import numpy as np
import ml_dtypes


def mxq(x, axis, fmt="e4m3"):
    dtype, down = {"e4m3": (ml_dtypes.float8_e4m3fn, 7), "e5m2": (ml_dtypes.float8_e5m2, 14)}[fmt]
    v = np.moveaxis(np.asarray(x, np.float32).astype(ml_dtypes.bfloat16).astype(np.float64), axis, -1)
    blocks = v.reshape(v.shape[:-1] + (-1, 32))
    amax = np.abs(blocks).max(-1, keepdims=True)
    byte = np.maximum(np.where(amax > 0, np.frexp(amax)[1] - 1 + 127, 0) - down, 1)
    scale = np.exp2(byte - 127.0)
    codes = (blocks / scale).astype(np.float32).astype(dtype).astype(np.float64)
    return np.moveaxis((codes * scale).reshape(v.shape), -1, axis)


WIDE = False


def mx_kscale(k):
    if not WIDE:
        return np.ones(k)
    levels = np.array([10, -10, 5, -5, 0])
    if k % 512:
        return np.exp2(np.random.permutation(np.resize(levels, k // 32))).repeat(32)
    a = np.empty((k // 512, 16))
    for p in range(k // 512):
        a[p, :8] = np.random.permutation(np.resize(levels, 8))
        for g in range(8):
            far = levels[np.abs(levels - a[p, g]) >= 10]
            a[p, g + 8] = far[np.random.randint(len(far))]
    return np.exp2(a.ravel()).repeat(32)


BF16 = ml_dtypes.bfloat16


def bf(x):
    return np.asarray(x, np.float32).astype(BF16)


def f64(x):
    return np.asarray(x).astype(np.float64)


E2M1 = np.array([0.0, 0.5, 1.0, 1.5, 2.0, 3.0, 4.0, 6.0, -0.0, -0.5, -1.0, -1.5, -2.0, -3.0, -4.0, -6.0])


def pack_weight(w, fmt):
    k, n = w.shape
    w = f64(bf(w)).reshape(k // 32, 32, n)
    amax = np.abs(w).max(1)
    if fmt == "e4m3":
        byte = np.frexp(amax)[1] - 1 + 127 - 7
    else:
        mant, ex = np.frexp(amax / 6.0)
        byte = np.where(mant > 0.5, ex, ex - 1) + 127
    byte = np.clip(np.where(amax > 0, byte, 1), 1, 254)
    scaled = (w * np.exp2(127.0 - byte)[:, None, :]).reshape(k, n).astype(np.float32)
    by_word = np.ascontiguousarray(scaled.reshape(k // 512, 128, 4, n).transpose(0, 1, 3, 2))
    if fmt == "e4m3":
        words = by_word.astype(ml_dtypes.float8_e4m3fn).view(np.uint8)
    else:
        c = by_word.astype(ml_dtypes.float4_e2m1fn).view(np.uint8) & 0xF
        words = c[..., 0::2] | (c[..., 1::2] << 4)
    return np.ascontiguousarray(words), np.ascontiguousarray(byte.astype(np.uint8).reshape(k // 512, 16, n))


def unpack_weight(words, scales, fmt):
    g, p, n, _ = words.shape
    if fmt == "e4m3":
        vals = np.ascontiguousarray(words).view(ml_dtypes.float8_e4m3fn).astype(np.float64)
    else:
        nib = np.empty((g, p, n, 4), np.uint8)
        nib[..., 0::2] = words & 0xF
        nib[..., 1::2] = words >> 4
        vals = E2M1[nib]
    vals = vals * np.repeat(np.exp2(scales.astype(np.float64) - 127.0), 8, axis=1)[..., None]
    return vals.transpose(0, 1, 3, 2).reshape(g * 512, n)
def pack4(w):
    words, scales = pack_weight(w, "e2m1")
    return words.reshape(words.shape[0], 128, -1), scales


def unpack4(words, scales):
    return unpack_weight(words.reshape(words.shape[0], 128, -1, 2), scales, "e2m1")


def planes(Y):
    n, m = Y.shape
    b = f64(bf(Y)).reshape(n // 32, 32, m)
    amax = np.abs(b).max(1)
    byte = np.clip(np.where(amax > 0, np.frexp(amax)[1] - 1 + 127 - 7, 1), 1, 254)
    codes = (b * np.exp2(127.0 - byte)[:, None, :]).reshape(n, m).astype(np.float32).astype(ml_dtypes.float8_e4m3fn).view(np.uint8)
    words = codes.reshape(n // 512, 128, 4, m).transpose(0, 1, 3, 2)
    return np.ascontiguousarray(words), np.ascontiguousarray(byte.astype(np.uint8).reshape(n // 512, 16, m))


P, S, Q, C = 1280, 1536, 1024, 1024
DRIFT = 0.04


def pair_differences(n, p):
    sd = np.sqrt(DRIFT * p * (1 - p))
    first = np.clip(p + sd * np.random.randn(n, S), 0, 1)
    second = np.clip(p + sd * np.random.randn(n, S), 0, 1)
    return first - second


def setup_inputs():
    s, t = mx_kscale(S), mx_kscale(Q)
    p = np.random.uniform(0.15, 0.85, S)
    het = 2 * p * (1 - p)
    left = pair_differences(P, p)
    right = pair_differences(Q, p)
    e_words, e_scales = pack4(right.T / s[:, None] * t[None, :])
    mix = np.random.randn(Q, Q) / (3 * np.sqrt(Q))
    combo = np.random.randn(Q, C) / np.sqrt(Q) * np.exp(0.8 * np.random.randn(C))
    return {
        "diff": bf(left),
        "snp_weight": bf(s / (3 * DRIFT * het * np.sqrt(S))),
        "e_words": e_words,
        "e_scales": e_scales,
        "table": bf(np.random.randn(P, Q) * t[None, :]),
        "mix": bf(mix / t[:, None] * t[None, :]),
        "combo": bf(combo / t[:, None]),
        "left_scale": bf(np.exp(0.3 * np.random.randn(P))),
        "offset": bf(0.3 * np.random.randn(C)),
    }


def reference(diff, snp_weight, e_words, e_scales, table, mix, combo, left_scale, offset):
    A = f64(diff) * f64(snp_weight)[None, :]
    E = unpack4(e_words, e_scales)
    T = f64(table) + (mxq(A, 1) @ E)
    U = T + (mxq(T, 1) @ mxq(f64(mix), 0))
    y = (mxq(U, 1) @ mxq(f64(combo), 0)) * f64(left_scale)[:, None] + f64(offset)[None, :]
    Y = y.T
    words, scales = planes(Y)
    return y, words, scales

@@ -1,0 +1,363 @@
+from contextlib import ExitStack
+
+import concourse.mybir as mybir
+from concourse.masks import make_identity
+
+F32 = mybir.dt.float32
+BF16 = mybir.dt.bfloat16
+I32 = mybir.dt.int32
+U32 = mybir.dt.uint32
+U8 = mybir.dt.uint8
+FP8X4 = mybir.dt.float8_e4m3fn_x4
+FP4X4 = mybir.dt.float4_e2m1fn_x4
+ALU = mybir.AluOpType
+
+ROWS, SNPS, PAIRS, COMBOS = 1280, 1536, 1024, 1024
+FLOPS = 2 * ROWS * PAIRS * (SNPS + PAIRS + COMBOS)
+
+P = 128
+PASS = 512
+BAND = 256
+BANDS = ROWS // BAND
+UNITS = 2 * BANDS
+SNP_GROUPS = SNPS // PASS
+GROUPS = PAIRS // PASS
+CHUNK = 256
+CHUNKS = GROUPS * PAIRS // CHUNK
+BANKS = 8
+
+STAGE1_STEP = 1
+STAGE2_STEP = 6
+STAGE3_STEP = 11
+MIX_STEP = 2
+COMBO_STEP = 7
+T_BUFS = 8
+T_ROUND = 1
+RATE = 4
+ORDER = "e0 m00 t0 d1 e1 m10 d2 t1 m01 m11 d3 t2 c00 c10 d4 t3 c01 c11 t4"
+SHARE_FROM = 7
+T_TURN, T_QUANT, U_TURN, U_QUANT, Y_TURN, Y_QUANT = 3, 3, 2, 3, 3, 4
+
+
+def tile_f4_table_update_k1_kernel(
+    tc, diff, snp_weight, e_words, e_scales, table, mix, combo, left_scale, offset, out_0, out_1, out_2
+):
+    nc = tc.nc
+    with ExitStack() as ctx:
+        keep = ctx.enter_context(tc.tile_pool(name="keep", bufs=1))
+        work = ctx.enter_context(tc.tile_pool(name="work", bufs=3))
+        psum = ctx.enter_context(tc.psum_pool(name="psum", bufs=1))
+        ctx.enter_context(tc.manual_schedule())
+
+        banks_taken = []
+
+        def new_bank():
+            name = "bank%d" % (len(banks_taken) % BANKS)
+            banks_taken.append(name)
+            return psum.tile([P, PASS], F32, name=name)
+
+        def band_rows(matrix, j):
+            return matrix[BAND * j : BAND * (j + 1), :].rearrange("(p h) c -> p h c", h=2)
+
+        def columns(n):
+            return slice(PASS * n, PASS * (n + 1))
+
+        def by_word_parity(ap):
+            return ap.rearrange("p (m u e) -> p u m e", u=2, e=2)
+
+        ident = keep.tile([P, P], F32, name="ident")
+        make_identity(nc, ident[:])
+        e_planes = keep.tile([P, SNP_GROUPS, PAIRS], U8, name="e_planes", align_bytes=64)
+        nc.vector.memset(e_planes[:].bitcast(I32), 0)
+
+        weight_sb = keep.tile([P, SNP_GROUPS, 4], BF16, name="weight_sb")
+        diff_sb, table_sb, e_codes, raw = {}, {}, {}, {}
+
+        def load_diff(j):
+            if j == 0:
+                for g in range(SNP_GROUPS):
+                    part = keep.tile([P, 2, PASS], BF16, name="diff_first%d" % g)
+                    nc.sync.dma_start(out=part[:], in_=band_rows(diff, j)[:, :, columns(g)])
+                    diff_sb[j, g] = part[:].bitcast(F32)
+            else:
+                whole = work.tile([P, 2, SNPS], BF16, name="diff_band", tag="rows", bufs=4)
+                nc.sync.dma_start(out=whole[:], in_=band_rows(diff, j))
+                for g in range(SNP_GROUPS):
+                    diff_sb[j, g] = whole[:, :, columns(g)].bitcast(F32)
+
+        def load_table(j):
+            table_sb[j] = keep.tile([P, 2, PAIRS], BF16, name="table%d" % j)
+            nc.sync.dma_start(out=table_sb[j][:], in_=band_rows(table, j))
+
+        def load_e_codes(n):
+            e_codes[n] = keep.tile([P, SNP_GROUPS, 2 * PASS], U8, name="e_codes%d" % n, align_bytes=64)
+            source = e_words.rearrange("g p b -> p g b")[:, :, 2 * PASS * n : 2 * PASS * (n + 1)]
+            nc.sync.dma_start(out=e_codes[n][:].bitcast(I32), in_=source.bitcast(I32))
+
+        def load_raw(name, matrix, g, n):
+            raw[name, g, n] = keep.tile([P, 4, PASS], BF16, name="%s_raw%d%d" % (name, g, n))
+            nc.sync.dma_start(
+                out=raw[name, g, n][:], in_=matrix[columns(g), columns(n)].rearrange("(p t) c -> p t c", t=4)
+            )
+
+        nc.sync.dma_start(out=weight_sb[:], in_=snp_weight.rearrange("(g p t) -> p g t", p=P, t=4))
+        load_diff(0)
+        for quadrant in range(4):
+            nc.sync.dma_start(
+                out=e_planes[32 * quadrant : 32 * quadrant + 4].bitcast(I32),
+                in_=e_scales[:, 4 * quadrant : 4 * quadrant + 4, :].rearrange("g r n -> r g n").bitcast(I32),
+            )
+        for item in ORDER.split():
+            if item[0] == "e":
+                load_e_codes(int(item[1]))
+            elif item[0] == "t":
+                load_table(int(item[1]))
+            elif item[0] == "d":
+                load_diff(int(item[1]))
+            elif item[0] == "m":
+                load_raw("mix", mix, int(item[1]), int(item[2]))
+            else:
+                load_raw("combo", combo, int(item[1]), int(item[2]))
+        scale_sb = keep.tile([P, BANDS, 2], BF16, name="scale_sb")
+        nc.sync.dma_start(out=scale_sb[:], in_=left_scale.rearrange("(j p h) -> p j h", p=P, h=2))
+        offset_sb = keep.tile([P, COMBOS], BF16, name="offset_sb")
+        nc.sync.dma_start(out=offset_sb[:], in_=offset.partition_broadcast(P))
+
+        def mx_tiles(pool, name, groups, width, bufs):
+            codes = pool.tile([P, groups, width], U32, name=name + "_codes", bufs=bufs, align_bytes=64)
+            scales = pool.tile([P, groups, width], U8, name=name + "_scales", bufs=bufs, align_bytes=64)
+            return codes, scales
+
+        def quantize(operand, g, cols, grouped):
+            codes, scales = operand
+            nc.vector.quantize_mx(out=codes[:, g, cols].bitcast(FP8X4), scales=scales[:, g, cols], in_=grouped[:])
+
+        weights_mx = {name: mx_tiles(keep, name, GROUPS, PAIRS, 1) for name in ("mix", "combo")}
+        y_mx = mx_tiles(keep, "y", GROUPS, ROWS, 1)
+        rows_mx = {}
+
+        def band_operand(name, j, groups, bufs):
+            if (name, j) not in rows_mx:
+                rows_mx[name, j] = mx_tiles(work, name, groups, BAND, bufs)
+            return rows_mx[name, j]
+
+        def new_grouped(tag):
+            return work.tile([P, 4 * BAND], BF16, name=tag, tag=tag, bufs=4, align_bytes=64)
+
+        held = {}
+
+        def interleave_weight(name, c):
+            n, g, c0 = c // 4, c // 2 % 2, c % 2 * CHUNK
+            grouped = new_grouped("weight_grouped")
+            nc.scalar.copy(
+                out=grouped[:].rearrange("p (c i t) -> p c t i", i=4, t=4),
+                in_=raw[name, g, n][:, :, c0 : c0 + CHUNK].rearrange("p t (c i) -> p c t i", i=4),
+            )
+            held[name, c] = grouped
+
+        def quantize_weight(name, c):
+            g, c0 = c // 2 % 2, c // 4 * PASS + c % 2 * CHUNK
+            quantize(weights_mx[name], g, slice(c0, c0 + CHUNK), held.pop((name, c)))
+
+        def turn_diff(j, g):
+            bank = new_bank()
+            quarters = bank[:].rearrange("p (u h r) -> p u h r", u=2, h=2)
+            for h in range(2):
+                for u in range(2):
+                    nc.tensor.transpose(quarters[:, u, h, :], diff_sb[j, g][:, h, u::2], ident[:])
+            held["a_bank", j, g] = bank
+
+        def weigh_diff(j, g):
+            bank = held.pop(("a_bank", j, g))
+            grouped = new_grouped("a_grouped")
+            nc.vector.tensor_tensor(
+                out=grouped[:].rearrange("p (r u e) -> p r u e", u=2, e=2),
+                in0=bank[:].bitcast(BF16).rearrange("p (u r e) -> p r u e", u=2, e=2),
+                in1=weight_sb[:, g, :].rearrange("p (u e) -> p u e", e=2).unsqueeze(1).to_broadcast([P, BAND, 2, 2]),
+                op=ALU.mult,
+            )
+            held["a_grouped", j, g] = grouped
+
+        def quantize_a(j, g):
+            quantize(band_operand("a", j, SNP_GROUPS, 2), g, slice(0, BAND), held.pop(("a_grouped", j, g)))
+
+        def multiply(stage, unit, rows_name, moving, groups):
+            j, n = divmod(unit, 2)
+            codes, scales = rows_mx[rows_name, j]
+            for h in range(2):
+                bank = new_bank()
+                for g in range(groups):
+                    rhs, rhs_scale = moving(g, n)
+                    nc.tensor.matmul_mx(
+                        out=bank[:],
+                        lhsT=codes[:, g, P * h : P * (h + 1)].bitcast(FP8X4),
+                        lhsT_scale=scales[:, g, P * h : P * (h + 1)],
+                        rhs=rhs,
+                        rhs_scale=rhs_scale,
+                        start=(g == 0),
+                        stop=(g == groups - 1),
+                    )
+                held[stage, unit, h] = bank
+
+        def e_operand(g, n):
+            return e_codes[n][:, g, :].bitcast(FP4X4), e_planes[:, g, columns(n)]
+
+        def weight_operand(name):
+            codes, scales = weights_mx[name]
+            return lambda g, n: (codes[:, g, columns(n)].bitcast(FP8X4), scales[:, g, columns(n)])
+
+        def new_rounded():
+            return work.tile([P, 2, PASS], BF16, name="rounded", bufs=6)
+
+        def sorted_view(ap):
+            return ap.rearrange("p (u m e) -> p u m e", u=2, e=2)
+
+        def add_table(unit):
+            j, n = divmod(unit, 2)
+            t_f32 = work.tile([P, 2, PASS], F32, name="t_f32", bufs=T_BUFS)
+            for h in range(2):
+                nc.vector.tensor_tensor(
+                    out=sorted_view(t_f32[:, h, :]),
+                    in0=by_word_parity(held.pop(("t", unit, h))[:]),
+                    in1=by_word_parity(table_sb[j][:, h, columns(n)]),
+                    op=ALU.add,
+                )
+            held["t_f32", unit] = t_f32
+
+        def round_t(unit):
+            rounded = new_rounded()
+            nc.scalar.copy(out=rounded[:], in_=held["t_f32", unit][:])
+            held["t_rounded", unit] = rounded
+
+        def add_t(unit):
+            t_f32 = held.pop(("t_f32", unit))
+            rounded = new_rounded()
+            for h in range(2):
+                nc.vector.tensor_tensor(
+                    out=sorted_view(rounded[:, h, :]),
+                    in0=by_word_parity(held.pop(("u", unit, h))[:]),
+                    in1=sorted_view(t_f32[:, h, :]),
+                    op=ALU.add,
+                )
+            held["u_rounded", unit] = rounded
+
+        def finish_y(unit):
+            j, n = divmod(unit, 2)
+            y_f32 = work.tile([P, 2, PASS], F32, name="y_f32", tag="rows", bufs=4)
+            for h in range(2):
+                nc.vector.scalar_tensor_tensor(
+                    out=y_f32[:, h, :],
+                    in0=held.pop(("y", unit, h))[:],
+                    scalar=scale_sb[:, j, h : h + 1],
+                    in1=offset_sb[:, columns(n)],
+                    op0=ALU.mult,
+                    op1=ALU.add,
+                )
+            nc.sync.dma_start(out=band_rows(out_0, j)[:, :, columns(n)], in_=y_f32[:])
+            held["y_f32", unit] = y_f32
+
+        def round_y(unit):
+            rounded = new_rounded()
+            y_f32 = held.pop(("y_f32", unit))
+            for h in range(2):
+                copy = nc.vector.tensor_copy if unit >= SHARE_FROM and h == 0 else nc.scalar.copy
+                copy(out=sorted_view(rounded[:, h, :]), in_=by_word_parity(y_f32[:, h, :]))
+            held["y_rounded", unit] = rounded
+
+        def turn(name, unit):
+            words = held.pop((name + "_rounded", unit))[:].bitcast(F32)
+            bank = new_bank()
+            quarters = bank[:].rearrange("p (u h r) -> p u h r", u=2, h=2)
+            for h in range(2):
+                for u in range(2):
+                    nc.tensor.transpose(quarters[:, u, h, :], words[:, h, P * u : P * (u + 1)], ident[:])
+            held[name + "_bank", unit] = bank
+
+        def group(name, unit):
+            bank = held.pop((name + "_bank", unit))
+            grouped = new_grouped("grouped")
+            if name == "y":
+                nc.scalar.copy(
+                    out=grouped[:].bitcast(F32).rearrange("p (r h u) -> p r h u", h=2, u=2),
+                    in_=bank[:].rearrange("p (u h r) -> p r h u", u=2, h=2),
+                )
+            else:
+                nc.scalar.copy(
+                    out=grouped[:].bitcast(F32).rearrange("p (r u) -> p r u", u=2),
+                    in_=bank[:].rearrange("p (u r) -> p r u", u=2),
+                )
+            held[name + "_grouped", unit] = grouped
+
+        def quantize_rows(name, unit, bufs):
+            j, n = divmod(unit, 2)
+            quantize(band_operand(name, j, GROUPS, bufs), n, slice(0, BAND), held.pop((name + "_grouped", unit)))
+
+        def quantize_y(unit):
+            j, n = divmod(unit, 2)
+            band = slice(BAND * j, BAND * (j + 1))
+            quantize(y_mx, n, band, held.pop(("y_grouped", unit)))
+            codes, scales = y_mx
+            nc.sync.dma_start(
+                out=out_1[n, :, band, :].rearrange("p m t -> p (m t)").bitcast(I32),
+                in_=codes[:, n, band].bitcast(I32),
+            )
+            if j == BANDS - 1:
+                for quadrant in range(4):
+                    nc.sync.dma_start(
+                        out=out_2[n, 4 * quadrant : 4 * quadrant + 4, :].bitcast(I32),
+                        in_=scales[32 * quadrant : 32 * quadrant + 4, n, :].bitcast(I32),
+                    )
+
+        def when_due(action, unit):
+            if 0 <= unit < UNITS:
+                action(unit)
+
+        def weight_chunks(step):
+            due = []
+            for name, first in (("mix", MIX_STEP), ("combo", COMBO_STEP)):
+                lo, hi = (RATE * (step - first) + 1) // 2, (RATE * (step - first + 1) + 1) // 2
+                due.extend((name, c) for c in range(max(lo, 0), min(hi, CHUNKS)))
+            return due
+
+        def diff_parts_done(step):
+            if step < 0:
+                return 0
+            return min(BANDS * SNP_GROUPS, SNP_GROUPS + (0 if step < 2 else SNP_GROUPS * step // 2))
+
+        for step in range(STAGE3_STEP + UNITS + Y_QUANT + 1):
+            diff_parts = [divmod(a, SNP_GROUPS) for a in range(diff_parts_done(step - 1), diff_parts_done(step))]
+            u1, u2, u3 = step - STAGE1_STEP, step - STAGE2_STEP, step - STAGE3_STEP
+
+            when_due(add_table, u1 - 1)
+            when_due(add_t, u2 - 1)
+            when_due(finish_y, u3 - 1)
+
+            when_due(lambda u: turn("y", u), u3 - Y_TURN)
+            when_due(lambda u: turn("u", u), u2 - U_TURN)
+            when_due(lambda u: turn("t", u), u1 - T_TURN)
+            for j, g in diff_parts:
+                turn_diff(j, g)
+
+            for name, c in weight_chunks(step)[:1]:
+                interleave_weight(name, c)
+            when_due(lambda u: group("y", u), u3 - Y_TURN)
+            when_due(lambda u: group("u", u), u2 - U_TURN)
+            when_due(lambda u: group("t", u), u1 - T_TURN)
+            when_due(round_t, u1 - T_ROUND)
+            when_due(round_y, u3 - 1)
+            for name, c in weight_chunks(step)[1:]:
+                interleave_weight(name, c)
+
+            for j, g in diff_parts:
+                weigh_diff(j, g)
+            for name, c in weight_chunks(step - 1):
+                quantize_weight(name, c)
+            when_due(quantize_y, u3 - Y_QUANT)
+            when_due(lambda u: quantize_rows("u", u, 3), u2 - U_QUANT)
+            when_due(lambda u: quantize_rows("t", u, 4), u1 - T_QUANT)
+            for j, g in diff_parts:
+                quantize_a(j, g)
+
+            when_due(lambda u: multiply("t", u, "a", e_operand, SNP_GROUPS), u1)
+            when_due(lambda u: multiply("u", u, "t", weight_operand("mix"), GROUPS), u2)
+            when_due(lambda u: multiply("y", u, "u", weight_operand("combo"), GROUPS), u3)

@@ -33,9 +33,14 @@ MIX_STEP = 2
 COMBO_STEP = 7
 T_BUFS = 8
 T_ROUND = 1
+POOL_ROUNDS = 8
+WARM = 0
+WARM2 = 0
+MIRROR_FROM, MIRROR_TO = 99, 99
+EARLY_BANDS = 3
 RATE = 4
-ORDER = "e0 m00 t0 d1 e1 m10 d2 t1 m01 m11 d3 t2 c00 c10 d4 t3 c01 c11 t4"
-SHARE_FROM = 7
+ORDER = "e0 d1 t0 e1 m00 d2 m10 t1 m01 d3 m11 t2 c00 d4 c10 t3 c01 c11 t4"
+SHARE_FROM = 8
 T_TURN, T_QUANT, U_TURN, U_QUANT, Y_TURN, Y_QUANT = 3, 3, 2, 3, 3, 4
 
 
@@ -69,6 +74,26 @@ def tile_f4_table_update_k1_kernel(
         make_identity(nc, ident[:])
         e_planes = keep.tile([P, SNP_GROUPS, PAIRS], U8, name="e_planes", align_bytes=64)
         nc.vector.memset(e_planes[:].bitcast(I32), 0)
+
+        if WARM:
+            ones = keep.tile([P, PASS], BF16, name="ones", align_bytes=64)
+            nc.vector.memset(ones[:], 1.0)
+            warm_codes = keep.tile([P, P], U32, name="warm_codes", align_bytes=64)
+            warm_scales = keep.tile([P, P], U8, name="warm_scales", align_bytes=64)
+            nc.vector.quantize_mx(out=warm_codes[:].bitcast(FP8X4), scales=warm_scales[:], in_=ones[:])
+
+        def warm(count):
+            bank = new_bank()
+            for i in range(count):
+                nc.tensor.matmul_mx(
+                    out=bank[:, P * (i % 4) : P * (i % 4 + 1)],
+                    lhsT=warm_codes[:].bitcast(FP8X4),
+                    lhsT_scale=warm_scales[:],
+                    rhs=warm_codes[:].bitcast(FP8X4),
+                    rhs_scale=warm_scales[:],
+                    start=True,
+                    stop=True,
+                )
 
         weight_sb = keep.tile([P, SNP_GROUPS, 4], BF16, name="weight_sb")
         diff_sb, table_sb, e_codes, raw = {}, {}, {}, {}
@@ -133,7 +158,13 @@ def tile_f4_table_update_k1_kernel(
             nc.vector.quantize_mx(out=codes[:, g, cols].bitcast(FP8X4), scales=scales[:, g, cols], in_=grouped[:])
 
         weights_mx = {name: mx_tiles(keep, name, GROUPS, PAIRS, 1) for name in ("mix", "combo")}
-        y_mx = mx_tiles(keep, "y", GROUPS, ROWS, 1)
+        y_codes = [
+            keep.tile([P, GROUPS, BAND], U32, name="y_codes%d" % j, align_bytes=64) for j in range(BANDS)
+        ]
+        y_scales = [
+            keep.tile([P, GROUPS, BAND * EARLY_BANDS], U8, name="y_scales_early", align_bytes=64),
+            keep.tile([P, GROUPS, BAND * (BANDS - EARLY_BANDS)], U8, name="y_scales_late", align_bytes=64),
+        ]
         rows_mx = {}
 
         def band_operand(name, j, groups, bufs):
@@ -215,6 +246,8 @@ def tile_f4_table_update_k1_kernel(
         def add_table(unit):
             j, n = divmod(unit, 2)
             t_f32 = work.tile([P, 2, PASS], F32, name="t_f32", bufs=T_BUFS)
+            if unit < POOL_ROUNDS:
+                held["t_rounded", unit] = new_rounded()
             for h in range(2):
                 nc.vector.tensor_tensor(
                     out=sorted_view(t_f32[:, h, :]),
@@ -222,9 +255,20 @@ def tile_f4_table_update_k1_kernel(
                     in1=by_word_parity(table_sb[j][:, h, columns(n)]),
                     op=ALU.add,
                 )
+                if unit < POOL_ROUNDS:
+                    nc.gpsimd.tensor_scalar(
+                        out=held["t_rounded", unit][:, h, :],
+                        in0=t_f32[:, h, :],
+                        scalar1=1.0,
+                        scalar2=0.0,
+                        op0=ALU.mult,
+                        op1=ALU.add,
+                    )
             held["t_f32", unit] = t_f32
 
         def round_t(unit):
+            if unit < POOL_ROUNDS:
+                return
             rounded = new_rounded()
             nc.scalar.copy(out=rounded[:], in_=held["t_f32", unit][:])
             held["t_rounded", unit] = rounded
@@ -294,18 +338,26 @@ def tile_f4_table_update_k1_kernel(
 
         def quantize_y(unit):
             j, n = divmod(unit, 2)
-            band = slice(BAND * j, BAND * (j + 1))
-            quantize(y_mx, n, band, held.pop(("y_grouped", unit)))
-            codes, scales = y_mx
-            nc.sync.dma_start(
-                out=out_1[n, :, band, :].rearrange("p m t -> p (m t)").bitcast(I32),
-                in_=codes[:, n, band].bitcast(I32),
+            late = j >= EARLY_BANDS
+            first = EARLY_BANDS if late else 0
+            last = BANDS if late else EARLY_BANDS
+            local = slice(BAND * (j - first), BAND * (j - first + 1))
+            codes, scales = y_codes[j], y_scales[late]
+            nc.vector.quantize_mx(
+                out=codes[:, n, :].bitcast(FP8X4), scales=scales[:, n, local], in_=held.pop(("y_grouped", unit))[:]
             )
-            if j == BANDS - 1:
+            if n == 1 or j == BANDS - 1:
+                groups_out = slice(n, n + 1) if j == BANDS - 1 else slice(0, GROUPS)
+                nc.sync.dma_start(
+                    out=out_1[groups_out, :, BAND * j : BAND * (j + 1), :].rearrange("g p m t -> p g (m t)").bitcast(I32),
+                    in_=codes[:, groups_out, :].bitcast(I32),
+                )
+            if n == 1 and j + 1 == last:
+                rows = slice(BAND * first, BAND * last)
                 for quadrant in range(4):
                     nc.sync.dma_start(
-                        out=out_2[n, 4 * quadrant : 4 * quadrant + 4, :].bitcast(I32),
-                        in_=scales[32 * quadrant : 32 * quadrant + 4, n, :].bitcast(I32),
+                        out=out_2[:, 4 * quadrant : 4 * quadrant + 4, rows].rearrange("g r m -> r g m").bitcast(I32),
+                        in_=scales[32 * quadrant : 32 * quadrant + 4].bitcast(I32),
                     )
 
         def when_due(action, unit):
@@ -324,40 +376,65 @@ def tile_f4_table_update_k1_kernel(
                 return 0
             return min(BANDS * SNP_GROUPS, SNP_GROUPS + (0 if step < 2 else SNP_GROUPS * step // 2))
 
-        for step in range(STAGE3_STEP + UNITS + Y_QUANT + 1):
-            diff_parts = [divmod(a, SNP_GROUPS) for a in range(diff_parts_done(step - 1), diff_parts_done(step))]
-            u1, u2, u3 = step - STAGE1_STEP, step - STAGE2_STEP, step - STAGE3_STEP
+        def diff_parts(step):
+            return [divmod(a, SNP_GROUPS) for a in range(diff_parts_done(step - 1), diff_parts_done(step))]
 
-            when_due(add_table, u1 - 1)
-            when_due(add_t, u2 - 1)
-            when_due(finish_y, u3 - 1)
+        def sums(step):
+            when_due(add_table, step - STAGE1_STEP)
+            when_due(add_t, step - STAGE2_STEP)
+            when_due(finish_y, step - STAGE3_STEP)
 
-            when_due(lambda u: turn("y", u), u3 - Y_TURN)
-            when_due(lambda u: turn("u", u), u2 - U_TURN)
-            when_due(lambda u: turn("t", u), u1 - T_TURN)
-            for j, g in diff_parts:
+        def turns(step):
+            when_due(lambda u: turn("y", u), step - STAGE3_STEP - Y_TURN)
+            when_due(lambda u: turn("u", u), step - STAGE2_STEP - U_TURN)
+            when_due(lambda u: turn("t", u), step - STAGE1_STEP - T_TURN)
+            for j, g in diff_parts(step):
                 turn_diff(j, g)
 
-            for name, c in weight_chunks(step)[:1]:
-                interleave_weight(name, c)
-            when_due(lambda u: group("y", u), u3 - Y_TURN)
-            when_due(lambda u: group("u", u), u2 - U_TURN)
-            when_due(lambda u: group("t", u), u1 - T_TURN)
-            when_due(round_t, u1 - T_ROUND)
-            when_due(round_y, u3 - 1)
-            for name, c in weight_chunks(step)[1:]:
-                interleave_weight(name, c)
+        def groups(step):
+            when_due(lambda u: group("y", u), step - STAGE3_STEP - Y_TURN)
+            when_due(lambda u: group("u", u), step - STAGE2_STEP - U_TURN)
+            when_due(lambda u: group("t", u), step - STAGE1_STEP - T_TURN)
 
-            for j, g in diff_parts:
-                weigh_diff(j, g)
+        def rounds(step):
+            when_due(round_t, step - STAGE1_STEP - T_ROUND)
+            when_due(round_y, step - STAGE3_STEP - 1)
+
+        def quantizes(step):
             for name, c in weight_chunks(step - 1):
                 quantize_weight(name, c)
-            when_due(quantize_y, u3 - Y_QUANT)
-            when_due(lambda u: quantize_rows("u", u, 3), u2 - U_QUANT)
-            when_due(lambda u: quantize_rows("t", u, 4), u1 - T_QUANT)
-            for j, g in diff_parts:
-                quantize_a(j, g)
+            when_due(quantize_y, step - STAGE3_STEP - Y_QUANT)
+            when_due(lambda u: quantize_rows("u", u, 3), step - STAGE2_STEP - U_QUANT)
+            when_due(lambda u: quantize_rows("t", u, 4), step - STAGE1_STEP - T_QUANT)
 
-            when_due(lambda u: multiply("t", u, "a", e_operand, SNP_GROUPS), u1)
-            when_due(lambda u: multiply("u", u, "t", weight_operand("mix"), GROUPS), u2)
-            when_due(lambda u: multiply("y", u, "u", weight_operand("combo"), GROUPS), u3)
+        def products(step):
+            when_due(lambda u: multiply("t", u, "a", e_operand, SNP_GROUPS), step - STAGE1_STEP)
+            when_due(lambda u: multiply("u", u, "t", weight_operand("mix"), GROUPS), step - STAGE2_STEP)
+            when_due(lambda u: multiply("y", u, "u", weight_operand("combo"), GROUPS), step - STAGE3_STEP)
+
+        if WARM:
+            warm(WARM)
+        for g in range(SNP_GROUPS):
+            turn_diff(0, g)
+            if WARM2 and g < 2:
+                warm(WARM2)
+            weigh_diff(0, g)
+            if g > 0:
+                quantize_a(0, g - 1)
+        quantize_a(0, SNP_GROUPS - 1)
+
+        for step in range(1, STAGE3_STEP + UNITS + Y_QUANT + 1):
+            sums(step - 1)
+            turns(step)
+            for name, c in weight_chunks(step)[:1]:
+                interleave_weight(name, c)
+            groups(step)
+            rounds(step)
+            for name, c in weight_chunks(step)[1:]:
+                interleave_weight(name, c)
+            for j, g in diff_parts(step):
+                weigh_diff(j, g)
+            quantizes(step)
+            for j, g in diff_parts(step):
+                quantize_a(j, g)
+            products(step)

@@ -12,36 +12,30 @@ FP8X4 = mybir.dt.float8_e4m3fn_x4
 FP4X4 = mybir.dt.float4_e2m1fn_x4
 ALU = mybir.AluOpType
 
-ROWS, SNPS, PAIRS, COMBOS = 1280, 1536, 1024, 1024
-FLOPS = 2 * ROWS * PAIRS * (SNPS + PAIRS + COMBOS)
+ROWS, SNPS, RIGHT, COMBOS = 1280, 1536, 1024, 1024
+FLOPS = 2 * ROWS * (SNPS * RIGHT + RIGHT * RIGHT + RIGHT * COMBOS)
 
 P = 128
-PASS = 512
-BAND = 256
+GROUP = 512
+BAND = 2 * P
+HALF = GROUP // 2
 BANDS = ROWS // BAND
-UNITS = 2 * BANDS
-SNP_GROUPS = SNPS // PASS
-GROUPS = PAIRS // PASS
-CHUNK = 256
-CHUNKS = GROUPS * PAIRS // CHUNK
+SNP_GROUPS = SNPS // GROUP
+GROUPS = RIGHT // GROUP
+UNITS = BANDS * GROUPS
+QUARTERS = GROUPS * GROUPS
+QUADRANTS = 4
 BANKS = 8
 
-STAGE1_STEP = 1
-STAGE2_STEP = 6
-STAGE3_STEP = 11
-MIX_STEP = 2
-COMBO_STEP = 7
-T_BUFS = 8
-T_ROUND = 1
-POOL_ROUNDS = 8
-WARM = 0
-WARM2 = 0
-MIRROR_FROM, MIRROR_TO = 99, 99
+SUM_LAG = 1
+TURN_LAG = {"t": 3, "u": 2, "y": 3}
+QUANTIZE_LAG = {"t": 3, "u": 3, "y": 4}
+T_STEP = 1
+U_STEP = T_STEP + GROUPS + QUANTIZE_LAG["t"]
+Y_STEP = U_STEP + GROUPS + QUANTIZE_LAG["u"]
+MIX_STEP, COMBO_STEP = U_STEP - QUARTERS, Y_STEP - QUARTERS
+LAST_BAND_UNIT = UNITS - GROUPS
 EARLY_BANDS = 3
-RATE = 4
-ORDER = "e0 d1 t0 e1 m00 d2 m10 t1 m01 d3 m11 t2 c00 d4 c10 t3 c01 c11 t4"
-SHARE_FROM = 8
-T_TURN, T_QUANT, U_TURN, U_QUANT, Y_TURN, Y_QUANT = 3, 3, 2, 3, 3, 4
 
 
 def tile_f4_table_update_k1_kernel(
@@ -50,7 +44,7 @@ def tile_f4_table_update_k1_kernel(
     nc = tc.nc
     with ExitStack() as ctx:
         keep = ctx.enter_context(tc.tile_pool(name="keep", bufs=1))
-        work = ctx.enter_context(tc.tile_pool(name="work", bufs=3))
+        work = ctx.enter_context(tc.tile_pool(name="work", bufs=1))
         psum = ctx.enter_context(tc.psum_pool(name="psum", bufs=1))
         ctx.enter_context(tc.manual_schedule())
 
@@ -59,92 +53,84 @@ def tile_f4_table_update_k1_kernel(
         def new_bank():
             name = "bank%d" % (len(banks_taken) % BANKS)
             banks_taken.append(name)
-            return psum.tile([P, PASS], F32, name=name)
+            return psum.tile([P, GROUP], F32, name=name)
 
         def band_rows(matrix, j):
             return matrix[BAND * j : BAND * (j + 1), :].rearrange("(p h) c -> p h c", h=2)
 
-        def columns(n):
-            return slice(PASS * n, PASS * (n + 1))
+        def group_span(g):
+            return slice(GROUP * g, GROUP * (g + 1))
 
-        def by_word_parity(ap):
+        def read_sorted(ap):
             return ap.rearrange("p (m u e) -> p u m e", u=2, e=2)
+
+        def lies_sorted(ap):
+            return ap.rearrange("p (u m e) -> p u m e", u=2, e=2)
+
+        def flat(ap):
+            return ap.rearrange("p a b -> p (a b)")
 
         ident = keep.tile([P, P], F32, name="ident")
         make_identity(nc, ident[:])
-        e_planes = keep.tile([P, SNP_GROUPS, PAIRS], U8, name="e_planes", align_bytes=64)
-        nc.vector.memset(e_planes[:].bitcast(I32), 0)
+        e_scale_sb = keep.tile([P, SNP_GROUPS, RIGHT], U8, name="e_scale_sb", align_bytes=64)
+        nc.vector.memset(e_scale_sb[:].bitcast(I32), 0)
 
-        if WARM:
-            ones = keep.tile([P, PASS], BF16, name="ones", align_bytes=64)
-            nc.vector.memset(ones[:], 1.0)
-            warm_codes = keep.tile([P, P], U32, name="warm_codes", align_bytes=64)
-            warm_scales = keep.tile([P, P], U8, name="warm_scales", align_bytes=64)
-            nc.vector.quantize_mx(out=warm_codes[:].bitcast(FP8X4), scales=warm_scales[:], in_=ones[:])
-
-        def warm(count):
-            bank = new_bank()
-            for i in range(count):
-                nc.tensor.matmul_mx(
-                    out=bank[:, P * (i % 4) : P * (i % 4 + 1)],
-                    lhsT=warm_codes[:].bitcast(FP8X4),
-                    lhsT_scale=warm_scales[:],
-                    rhs=warm_codes[:].bitcast(FP8X4),
-                    rhs_scale=warm_scales[:],
-                    start=True,
-                    stop=True,
-                )
-
-        weight_sb = keep.tile([P, SNP_GROUPS, 4], BF16, name="weight_sb")
-        diff_sb, table_sb, e_codes, raw = {}, {}, {}, {}
+        diff_twins, table_sb, e_codes, weight_rows = {}, {}, {}, {}
 
         def load_diff(j):
-            if j == 0:
-                for g in range(SNP_GROUPS):
-                    part = keep.tile([P, 2, PASS], BF16, name="diff_first%d" % g)
-                    nc.sync.dma_start(out=part[:], in_=band_rows(diff, j)[:, :, columns(g)])
-                    diff_sb[j, g] = part[:].bitcast(F32)
-            else:
-                whole = work.tile([P, 2, SNPS], BF16, name="diff_band", tag="rows", bufs=4)
-                nc.sync.dma_start(out=whole[:], in_=band_rows(diff, j))
-                for g in range(SNP_GROUPS):
-                    diff_sb[j, g] = whole[:, :, columns(g)].bitcast(F32)
+            band = work.tile([P, 2, SNPS], BF16, name="diff_band", tag="rows", bufs=4)
+            nc.sync.dma_start(out=band[:], in_=band_rows(diff, j))
+            for g in range(SNP_GROUPS):
+                diff_twins[j, g] = band[:, :, group_span(g)].bitcast(F32)
+
+        def load_first_diff(g):
+            part = keep.tile([P, 2, GROUP], BF16, name="diff_first%d" % g)
+            nc.sync.dma_start(out=part[:], in_=band_rows(diff, 0)[:, :, group_span(g)])
+            diff_twins[0, g] = part[:].bitcast(F32)
 
         def load_table(j):
-            table_sb[j] = keep.tile([P, 2, PAIRS], BF16, name="table%d" % j)
+            table_sb[j] = keep.tile([P, 2, RIGHT], BF16, name="table%d" % j)
             nc.sync.dma_start(out=table_sb[j][:], in_=band_rows(table, j))
 
         def load_e_codes(n):
-            e_codes[n] = keep.tile([P, SNP_GROUPS, 2 * PASS], U8, name="e_codes%d" % n, align_bytes=64)
-            source = e_words.rearrange("g p b -> p g b")[:, :, 2 * PASS * n : 2 * PASS * (n + 1)]
+            e_codes[n] = keep.tile([P, SNP_GROUPS, 2 * GROUP], U8, name="e_codes%d" % n, align_bytes=64)
+            source = e_words.rearrange("g p b -> p g b")[:, :, 2 * GROUP * n : 2 * GROUP * (n + 1)]
             nc.sync.dma_start(out=e_codes[n][:].bitcast(I32), in_=source.bitcast(I32))
 
-        def load_raw(name, matrix, g, n):
-            raw[name, g, n] = keep.tile([P, 4, PASS], BF16, name="%s_raw%d%d" % (name, g, n))
-            nc.sync.dma_start(
-                out=raw[name, g, n][:], in_=matrix[columns(g), columns(n)].rearrange("(p t) c -> p t c", t=4)
-            )
+        def load_quarter(name, matrix, quarter):
+            n, g = divmod(quarter, GROUPS)
+            rows = keep.tile([P, 4, GROUP], BF16, name="%s_rows%d" % (name, quarter))
+            nc.sync.dma_start(out=rows[:], in_=matrix[group_span(g), group_span(n)].rearrange("(p t) c -> p t c", t=4))
+            weight_rows[name, quarter] = rows
 
-        nc.sync.dma_start(out=weight_sb[:], in_=snp_weight.rearrange("(g p t) -> p g t", p=P, t=4))
-        load_diff(0)
-        for quadrant in range(4):
+        snp_weight_sb = keep.tile([P, SNP_GROUPS, 4], BF16, name="snp_weight_sb")
+        nc.sync.dma_start(out=snp_weight_sb[:], in_=snp_weight.rearrange("(g p t) -> p g t", p=P, t=4))
+        for g in range(SNP_GROUPS):
+            load_first_diff(g)
+        for q in range(QUADRANTS):
             nc.sync.dma_start(
-                out=e_planes[32 * quadrant : 32 * quadrant + 4].bitcast(I32),
-                in_=e_scales[:, 4 * quadrant : 4 * quadrant + 4, :].rearrange("g r n -> r g n").bitcast(I32),
+                out=e_scale_sb[32 * q : 32 * q + 4].bitcast(I32),
+                in_=e_scales[:, 4 * q : 4 * q + 4, :].rearrange("g r n -> r g n").bitcast(I32),
             )
-        for item in ORDER.split():
-            if item[0] == "e":
-                load_e_codes(int(item[1]))
-            elif item[0] == "t":
-                load_table(int(item[1]))
-            elif item[0] == "d":
-                load_diff(int(item[1]))
-            elif item[0] == "m":
-                load_raw("mix", mix, int(item[1]), int(item[2]))
-            else:
-                load_raw("combo", combo, int(item[1]), int(item[2]))
-        scale_sb = keep.tile([P, BANDS, 2], BF16, name="scale_sb")
-        nc.sync.dma_start(out=scale_sb[:], in_=left_scale.rearrange("(j p h) -> p j h", p=P, h=2))
+        load_e_codes(0)
+        load_diff(1)
+        load_table(0)
+        load_e_codes(1)
+        row_loads = []
+        for j in range(1, BANDS):
+            if j + 1 < BANDS:
+                row_loads.append((load_diff, j + 1))
+            row_loads.append((load_table, j))
+        quarter_loads = [
+            (name, matrix, quarter) for name, matrix in (("mix", mix), ("combo", combo)) for quarter in range(QUARTERS)
+        ]
+        for i, (name, matrix, quarter) in enumerate(quarter_loads):
+            load_quarter(name, matrix, quarter)
+            if i < len(row_loads):
+                load_rows, j = row_loads[i]
+                load_rows(j)
+        left_scale_sb = keep.tile([P, BANDS, 2], BF16, name="left_scale_sb")
+        nc.sync.dma_start(out=left_scale_sb[:], in_=left_scale.rearrange("(j p h) -> p j h", p=P, h=2))
         offset_sb = keep.tile([P, COMBOS], BF16, name="offset_sb")
         nc.sync.dma_start(out=offset_sb[:], in_=offset.partition_broadcast(P))
 
@@ -153,68 +139,64 @@ def tile_f4_table_update_k1_kernel(
             scales = pool.tile([P, groups, width], U8, name=name + "_scales", bufs=bufs, align_bytes=64)
             return codes, scales
 
-        def quantize(operand, g, cols, grouped):
-            codes, scales = operand
-            nc.vector.quantize_mx(out=codes[:, g, cols].bitcast(FP8X4), scales=scales[:, g, cols], in_=grouped[:])
+        def quantize(codes, scales, grouped):
+            nc.vector.quantize_mx(out=flat(codes).bitcast(FP8X4), scales=flat(scales), in_=flat(grouped))
 
-        weights_mx = {name: mx_tiles(keep, name, GROUPS, PAIRS, 1) for name in ("mix", "combo")}
-        y_codes = [
-            keep.tile([P, GROUPS, BAND], U32, name="y_codes%d" % j, align_bytes=64) for j in range(BANDS)
-        ]
+        def new_grouped(name, parts, bufs):
+            return work.tile([P, parts, 4 * BAND], BF16, name=name, bufs=bufs, align_bytes=64)
+
+        def new_rounded():
+            return work.tile([P, 2, GROUP], BF16, name="rounded", bufs=6)
+
+        weight_mx = {name: mx_tiles(keep, name, GROUPS, RIGHT, 1) for name in ("mix", "combo")}
+        y_codes = [keep.tile([P, GROUPS, BAND], U32, name="y_codes%d" % j, align_bytes=64) for j in range(BANDS)]
         y_scales = [
             keep.tile([P, GROUPS, BAND * EARLY_BANDS], U8, name="y_scales_early", align_bytes=64),
             keep.tile([P, GROUPS, BAND * (BANDS - EARLY_BANDS)], U8, name="y_scales_late", align_bytes=64),
         ]
-        rows_mx = {}
-
-        def band_operand(name, j, groups, bufs):
-            if (name, j) not in rows_mx:
-                rows_mx[name, j] = mx_tiles(work, name, groups, BAND, bufs)
-            return rows_mx[name, j]
-
-        def new_grouped(tag):
-            return work.tile([P, 4 * BAND], BF16, name=tag, tag=tag, bufs=4, align_bytes=64)
-
+        band_mx = {}
         held = {}
 
-        def interleave_weight(name, c):
-            n, g, c0 = c // 4, c // 2 % 2, c % 2 * CHUNK
-            grouped = new_grouped("weight_grouped")
+        def group_weight(name, quarter, half):
+            if half == 0:
+                held[name, quarter] = new_grouped("weight_grouped", 2, 3)
             nc.scalar.copy(
-                out=grouped[:].rearrange("p (c i t) -> p c t i", i=4, t=4),
-                in_=raw[name, g, n][:, :, c0 : c0 + CHUNK].rearrange("p t (c i) -> p c t i", i=4),
+                out=held[name, quarter][:, half, :].rearrange("p (c i t) -> p c t i", i=4, t=4),
+                in_=weight_rows[name, quarter][:, :, HALF * half : HALF * (half + 1)].rearrange("p t (c i) -> p c t i", i=4),
             )
-            held[name, c] = grouped
 
-        def quantize_weight(name, c):
-            g, c0 = c // 2 % 2, c // 4 * PASS + c % 2 * CHUNK
-            quantize(weights_mx[name], g, slice(c0, c0 + CHUNK), held.pop((name, c)))
+        def quantize_weight(name, quarter):
+            n, g = divmod(quarter, GROUPS)
+            codes, scales = weight_mx[name]
+            quantize(codes[:, g : g + 1, group_span(n)], scales[:, g : g + 1, group_span(n)], held.pop((name, quarter))[:])
 
         def turn_diff(j, g):
             bank = new_bank()
-            quarters = bank[:].rearrange("p (u h r) -> p u h r", u=2, h=2)
+            outputs = bank[:].rearrange("p (u h r) -> p u h r", u=2, h=2)
             for h in range(2):
                 for u in range(2):
-                    nc.tensor.transpose(quarters[:, u, h, :], diff_sb[j, g][:, h, u::2], ident[:])
+                    nc.tensor.transpose(outputs[:, u, h, :], diff_twins[j, g][:, h, u::2], ident[:])
             held["a_bank", j, g] = bank
 
         def weigh_diff(j, g):
-            bank = held.pop(("a_bank", j, g))
-            grouped = new_grouped("a_grouped")
+            if g == 0:
+                held["a_grouped", j] = new_grouped("a_grouped", SNP_GROUPS, 2)
             nc.vector.tensor_tensor(
-                out=grouped[:].rearrange("p (r u e) -> p r u e", u=2, e=2),
-                in0=bank[:].bitcast(BF16).rearrange("p (u r e) -> p r u e", u=2, e=2),
-                in1=weight_sb[:, g, :].rearrange("p (u e) -> p u e", e=2).unsqueeze(1).to_broadcast([P, BAND, 2, 2]),
+                out=held["a_grouped", j][:, g, :].rearrange("p (r u e) -> p r u e", u=2, e=2),
+                in0=held.pop(("a_bank", j, g))[:].bitcast(BF16).rearrange("p (u r e) -> p r u e", u=2, e=2),
+                in1=snp_weight_sb[:, g, :].rearrange("p (u e) -> p u e", e=2).unsqueeze(1).to_broadcast([P, BAND, 2, 2]),
                 op=ALU.mult,
             )
-            held["a_grouped", j, g] = grouped
 
-        def quantize_a(j, g):
-            quantize(band_operand("a", j, SNP_GROUPS, 2), g, slice(0, BAND), held.pop(("a_grouped", j, g)))
+        def quantize_a(j, first, last):
+            if first == 0:
+                band_mx["a", j] = mx_tiles(work, "a", SNP_GROUPS, BAND, 2)
+            codes, scales = band_mx["a", j]
+            quantize(codes[:, first:last, :], scales[:, first:last, :], held["a_grouped", j][:, first:last, :])
 
-        def multiply(stage, unit, rows_name, moving, groups):
-            j, n = divmod(unit, 2)
-            codes, scales = rows_mx[rows_name, j]
+        def multiply(result, unit, stationary, moving, groups):
+            j, n = divmod(unit, GROUPS)
+            codes, scales = band_mx[stationary, j]
             for h in range(2):
                 bank = new_bank()
                 for g in range(groups):
@@ -228,213 +210,208 @@ def tile_f4_table_update_k1_kernel(
                         start=(g == 0),
                         stop=(g == groups - 1),
                     )
-                held[stage, unit, h] = bank
+                held[result, unit, h] = bank
 
         def e_operand(g, n):
-            return e_codes[n][:, g, :].bitcast(FP4X4), e_planes[:, g, columns(n)]
+            return e_codes[n][:, g, :].bitcast(FP4X4), e_scale_sb[:, g, group_span(n)]
 
         def weight_operand(name):
-            codes, scales = weights_mx[name]
-            return lambda g, n: (codes[:, g, columns(n)].bitcast(FP8X4), scales[:, g, columns(n)])
+            codes, scales = weight_mx[name]
+            return lambda g, n: (codes[:, g, group_span(n)].bitcast(FP8X4), scales[:, g, group_span(n)])
 
-        def new_rounded():
-            return work.tile([P, 2, PASS], BF16, name="rounded", bufs=6)
-
-        def sorted_view(ap):
-            return ap.rearrange("p (u m e) -> p u m e", u=2, e=2)
-
-        def add_table(unit):
-            j, n = divmod(unit, 2)
-            t_f32 = work.tile([P, 2, PASS], F32, name="t_f32", bufs=T_BUFS)
-            if unit < POOL_ROUNDS:
-                held["t_rounded", unit] = new_rounded()
+        def sum_t(unit):
+            j, n = divmod(unit, GROUPS)
+            t_f32 = work.tile([P, 2, GROUP], F32, name="t_f32", bufs=U_STEP - T_STEP + 2)
+            rounded = new_rounded()
             for h in range(2):
                 nc.vector.tensor_tensor(
-                    out=sorted_view(t_f32[:, h, :]),
-                    in0=by_word_parity(held.pop(("t", unit, h))[:]),
-                    in1=by_word_parity(table_sb[j][:, h, columns(n)]),
+                    out=lies_sorted(t_f32[:, h, :]),
+                    in0=read_sorted(held.pop(("t", unit, h))[:]),
+                    in1=read_sorted(table_sb[j][:, h, group_span(n)]),
                     op=ALU.add,
                 )
-                if unit < POOL_ROUNDS:
+                if gpsimd_rounds(unit, h):
                     nc.gpsimd.tensor_scalar(
-                        out=held["t_rounded", unit][:, h, :],
-                        in0=t_f32[:, h, :],
-                        scalar1=1.0,
-                        scalar2=0.0,
-                        op0=ALU.mult,
-                        op1=ALU.add,
+                        out=rounded[:, h, :], in0=t_f32[:, h, :], scalar1=1.0, scalar2=0.0, op0=ALU.mult, op1=ALU.add
                     )
             held["t_f32", unit] = t_f32
-
-        def round_t(unit):
-            if unit < POOL_ROUNDS:
-                return
-            rounded = new_rounded()
-            nc.scalar.copy(out=rounded[:], in_=held["t_f32", unit][:])
             held["t_rounded", unit] = rounded
 
-        def add_t(unit):
+        def gpsimd_rounds(unit, h):
+            step = T_STEP + unit + SUM_LAG
+            covered = h == 0 or step > U_STEP or len(diff_groups_due(step)) > 1
+            return unit < LAST_BAND_UNIT and covered
+
+        def round_t_on_scalar(unit):
+            for h in range(2):
+                if not gpsimd_rounds(unit, h):
+                    nc.scalar.copy(out=held["t_rounded", unit][:, h, :], in_=held["t_f32", unit][:, h, :])
+
+        def sum_u(unit):
             t_f32 = held.pop(("t_f32", unit))
             rounded = new_rounded()
             for h in range(2):
                 nc.vector.tensor_tensor(
-                    out=sorted_view(rounded[:, h, :]),
-                    in0=by_word_parity(held.pop(("u", unit, h))[:]),
-                    in1=sorted_view(t_f32[:, h, :]),
+                    out=lies_sorted(rounded[:, h, :]),
+                    in0=read_sorted(held.pop(("u", unit, h))[:]),
+                    in1=lies_sorted(t_f32[:, h, :]),
                     op=ALU.add,
                 )
             held["u_rounded", unit] = rounded
 
-        def finish_y(unit):
-            j, n = divmod(unit, 2)
-            y_f32 = work.tile([P, 2, PASS], F32, name="y_f32", tag="rows", bufs=4)
+        def sum_y(unit):
+            j, n = divmod(unit, GROUPS)
+            y_f32 = work.tile([P, 2, GROUP], F32, name="y_f32", tag="rows", bufs=4)
             for h in range(2):
                 nc.vector.scalar_tensor_tensor(
                     out=y_f32[:, h, :],
                     in0=held.pop(("y", unit, h))[:],
-                    scalar=scale_sb[:, j, h : h + 1],
-                    in1=offset_sb[:, columns(n)],
+                    scalar=left_scale_sb[:, j, h : h + 1],
+                    in1=offset_sb[:, group_span(n)],
                     op0=ALU.mult,
                     op1=ALU.add,
                 )
-            nc.sync.dma_start(out=band_rows(out_0, j)[:, :, columns(n)], in_=y_f32[:])
+            nc.sync.dma_start(out=band_rows(out_0, j)[:, :, group_span(n)], in_=y_f32[:])
             held["y_f32", unit] = y_f32
 
-        def round_y(unit):
-            rounded = new_rounded()
-            y_f32 = held.pop(("y_f32", unit))
-            for h in range(2):
-                copy = nc.vector.tensor_copy if unit >= SHARE_FROM and h == 0 else nc.scalar.copy
-                copy(out=sorted_view(rounded[:, h, :]), in_=by_word_parity(y_f32[:, h, :]))
-            held["y_rounded", unit] = rounded
+        def round_y(copy, unit, h):
+            copy(out=lies_sorted(held["y_rounded", unit][:, h, :]), in_=read_sorted(held["y_f32", unit][:, h, :]))
+
+        def round_y_on_scalar(unit):
+            held["y_rounded", unit] = new_rounded()
+            round_y(nc.scalar.copy, unit, 0)
+            if unit < LAST_BAND_UNIT:
+                round_y(nc.scalar.copy, unit, 1)
+
+        def round_y_on_vector(unit):
+            if unit >= LAST_BAND_UNIT:
+                round_y(nc.vector.tensor_copy, unit, 1)
 
         def turn(name, unit):
-            words = held.pop((name + "_rounded", unit))[:].bitcast(F32)
+            twins = held.pop((name + "_rounded", unit))[:].bitcast(F32)
             bank = new_bank()
-            quarters = bank[:].rearrange("p (u h r) -> p u h r", u=2, h=2)
+            outputs = bank[:].rearrange("p (u h r) -> p u h r", u=2, h=2)
             for h in range(2):
                 for u in range(2):
-                    nc.tensor.transpose(quarters[:, u, h, :], words[:, h, P * u : P * (u + 1)], ident[:])
+                    nc.tensor.transpose(outputs[:, u, h, :], twins[:, h, P * u : P * (u + 1)], ident[:])
             held[name + "_bank", unit] = bank
 
-        def group(name, unit):
-            bank = held.pop((name + "_bank", unit))
-            grouped = new_grouped("grouped")
-            if name == "y":
-                nc.scalar.copy(
-                    out=grouped[:].bitcast(F32).rearrange("p (r h u) -> p r h u", h=2, u=2),
-                    in_=bank[:].rearrange("p (u h r) -> p r h u", u=2, h=2),
-                )
-            else:
-                nc.scalar.copy(
-                    out=grouped[:].bitcast(F32).rearrange("p (r u) -> p r u", u=2),
-                    in_=bank[:].rearrange("p (u r) -> p r u", u=2),
-                )
-            held[name + "_grouped", unit] = grouped
+        def group_rows(name, unit):
+            j, n = divmod(unit, GROUPS)
+            if n == 0:
+                held[name + "_grouped", j] = new_grouped(name + "_grouped", GROUPS, 2)
+            nc.scalar.copy(
+                out=held[name + "_grouped", j][:, n, :].bitcast(F32).rearrange("p (r u) -> p r u", u=2),
+                in_=held.pop((name + "_bank", unit))[:].rearrange("p (u r) -> p r u", u=2),
+            )
 
-        def quantize_rows(name, unit, bufs):
-            j, n = divmod(unit, 2)
-            quantize(band_operand(name, j, GROUPS, bufs), n, slice(0, BAND), held.pop((name + "_grouped", unit)))
+        def group_y(unit):
+            grouped = new_grouped("y_grouped", 1, 3)
+            nc.scalar.copy(
+                out=grouped[:, 0, :].bitcast(F32).rearrange("p (r h u) -> p r h u", h=2, u=2),
+                in_=held.pop(("y_bank", unit))[:].rearrange("p (u h r) -> p r h u", u=2, h=2),
+            )
+            held["y_grouped", unit] = grouped
+
+        def quantize_rows(name, unit):
+            j, n = divmod(unit, GROUPS)
+            if n == GROUPS - 1:
+                band_mx[name, j] = mx_tiles(work, name, GROUPS, BAND, 3)
+                codes, scales = band_mx[name, j]
+                quantize(codes[:], scales[:], held.pop((name + "_grouped", j))[:])
+
+        def store_y_codes(j, first, last):
+            nc.sync.dma_start(
+                out=out_1[first:last, :, BAND * j : BAND * (j + 1), :].rearrange("g p m t -> p g (m t)").bitcast(I32),
+                in_=y_codes[j][:, first:last, :].bitcast(I32),
+            )
 
         def quantize_y(unit):
-            j, n = divmod(unit, 2)
+            j, n = divmod(unit, GROUPS)
             late = j >= EARLY_BANDS
-            first = EARLY_BANDS if late else 0
-            last = BANDS if late else EARLY_BANDS
-            local = slice(BAND * (j - first), BAND * (j - first + 1))
-            codes, scales = y_codes[j], y_scales[late]
-            nc.vector.quantize_mx(
-                out=codes[:, n, :].bitcast(FP8X4), scales=scales[:, n, local], in_=held.pop(("y_grouped", unit))[:]
+            first, last = (EARLY_BANDS, BANDS) if late else (0, EARLY_BANDS)
+            scales = y_scales[late]
+            quantize(
+                y_codes[j][:, n : n + 1, :],
+                scales[:, n : n + 1, BAND * (j - first) : BAND * (j - first + 1)],
+                held.pop(("y_grouped", unit))[:],
             )
-            if n == 1 or j == BANDS - 1:
-                groups_out = slice(n, n + 1) if j == BANDS - 1 else slice(0, GROUPS)
-                nc.sync.dma_start(
-                    out=out_1[groups_out, :, BAND * j : BAND * (j + 1), :].rearrange("g p m t -> p g (m t)").bitcast(I32),
-                    in_=codes[:, groups_out, :].bitcast(I32),
-                )
-            if n == 1 and j + 1 == last:
+            if j == BANDS - 1:
+                store_y_codes(j, n, n + 1)
+            elif n == GROUPS - 1:
+                store_y_codes(j, 0, GROUPS)
+            if n == GROUPS - 1 and j + 1 == last:
                 rows = slice(BAND * first, BAND * last)
-                for quadrant in range(4):
+                for q in range(QUADRANTS):
                     nc.sync.dma_start(
-                        out=out_2[:, 4 * quadrant : 4 * quadrant + 4, rows].rearrange("g r m -> r g m").bitcast(I32),
-                        in_=scales[32 * quadrant : 32 * quadrant + 4].bitcast(I32),
+                        out=out_2[:, 4 * q : 4 * q + 4, rows].rearrange("g r m -> r g m").bitcast(I32),
+                        in_=scales[32 * q : 32 * q + 4].bitcast(I32),
                     )
 
         def when_due(action, unit):
             if 0 <= unit < UNITS:
                 action(unit)
 
-        def weight_chunks(step):
-            due = []
-            for name, first in (("mix", MIX_STEP), ("combo", COMBO_STEP)):
-                lo, hi = (RATE * (step - first) + 1) // 2, (RATE * (step - first + 1) + 1) // 2
-                due.extend((name, c) for c in range(max(lo, 0), min(hi, CHUNKS)))
-            return due
+        def quarters_due(step):
+            starts = (("mix", MIX_STEP), ("combo", COMBO_STEP))
+            return [(name, step - first) for name, first in starts if 0 <= step - first < QUARTERS]
 
-        def diff_parts_done(step):
-            if step < 0:
-                return 0
-            return min(BANDS * SNP_GROUPS, SNP_GROUPS + (0 if step < 2 else SNP_GROUPS * step // 2))
+        def diff_groups_due(step):
+            j, early = (step + 1) // 2, step % 2 == 1
+            if not 1 <= j < BANDS:
+                return []
+            if j == 1:
+                return [] if early else [(j, 0), (j, 1), (j, 2)]
+            return [(j, 0)] if early else [(j, 1), (j, 2)]
 
-        def diff_parts(step):
-            return [divmod(a, SNP_GROUPS) for a in range(diff_parts_done(step - 1), diff_parts_done(step))]
-
-        def sums(step):
-            when_due(add_table, step - STAGE1_STEP)
-            when_due(add_t, step - STAGE2_STEP)
-            when_due(finish_y, step - STAGE3_STEP)
-
-        def turns(step):
-            when_due(lambda u: turn("y", u), step - STAGE3_STEP - Y_TURN)
-            when_due(lambda u: turn("u", u), step - STAGE2_STEP - U_TURN)
-            when_due(lambda u: turn("t", u), step - STAGE1_STEP - T_TURN)
-            for j, g in diff_parts(step):
-                turn_diff(j, g)
-
-        def groups(step):
-            when_due(lambda u: group("y", u), step - STAGE3_STEP - Y_TURN)
-            when_due(lambda u: group("u", u), step - STAGE2_STEP - U_TURN)
-            when_due(lambda u: group("t", u), step - STAGE1_STEP - T_TURN)
-
-        def rounds(step):
-            when_due(round_t, step - STAGE1_STEP - T_ROUND)
-            when_due(round_y, step - STAGE3_STEP - 1)
-
-        def quantizes(step):
-            for name, c in weight_chunks(step - 1):
-                quantize_weight(name, c)
-            when_due(quantize_y, step - STAGE3_STEP - Y_QUANT)
-            when_due(lambda u: quantize_rows("u", u, 3), step - STAGE2_STEP - U_QUANT)
-            when_due(lambda u: quantize_rows("t", u, 4), step - STAGE1_STEP - T_QUANT)
-
-        def products(step):
-            when_due(lambda u: multiply("t", u, "a", e_operand, SNP_GROUPS), step - STAGE1_STEP)
-            when_due(lambda u: multiply("u", u, "t", weight_operand("mix"), GROUPS), step - STAGE2_STEP)
-            when_due(lambda u: multiply("y", u, "u", weight_operand("combo"), GROUPS), step - STAGE3_STEP)
-
-        if WARM:
-            warm(WARM)
         for g in range(SNP_GROUPS):
             turn_diff(0, g)
-            if WARM2 and g < 2:
-                warm(WARM2)
             weigh_diff(0, g)
             if g > 0:
-                quantize_a(0, g - 1)
-        quantize_a(0, SNP_GROUPS - 1)
+                quantize_a(0, g - 1, g)
+        quantize_a(0, SNP_GROUPS - 1, SNP_GROUPS)
 
-        for step in range(1, STAGE3_STEP + UNITS + Y_QUANT + 1):
-            sums(step - 1)
-            turns(step)
-            for name, c in weight_chunks(step)[:1]:
-                interleave_weight(name, c)
-            groups(step)
-            rounds(step)
-            for name, c in weight_chunks(step)[1:]:
-                interleave_weight(name, c)
-            for j, g in diff_parts(step):
+        for step in range(T_STEP, Y_STEP + UNITS + QUANTIZE_LAG["y"]):
+            t_unit, u_unit, y_unit = step - T_STEP, step - U_STEP, step - Y_STEP
+
+            when_due(sum_t, t_unit - SUM_LAG)
+            when_due(sum_u, u_unit - SUM_LAG)
+            when_due(sum_y, y_unit - SUM_LAG)
+
+            when_due(lambda unit: turn("y", unit), y_unit - TURN_LAG["y"])
+            when_due(lambda unit: turn("u", unit), u_unit - TURN_LAG["u"])
+            when_due(lambda unit: turn("t", unit), t_unit - TURN_LAG["t"])
+            for j, g in diff_groups_due(step):
+                turn_diff(j, g)
+
+            round_y_first = y_unit - SUM_LAG >= LAST_BAND_UNIT
+            for name, quarter in quarters_due(step):
+                group_weight(name, quarter, 0)
+            if round_y_first:
+                when_due(round_y_on_scalar, y_unit - SUM_LAG)
+            when_due(group_y, y_unit - TURN_LAG["y"])
+            when_due(lambda unit: group_rows("u", unit), u_unit - TURN_LAG["u"])
+            when_due(lambda unit: group_rows("t", unit), t_unit - TURN_LAG["t"])
+            when_due(round_t_on_scalar, t_unit - SUM_LAG)
+            if not round_y_first:
+                when_due(round_y_on_scalar, y_unit - SUM_LAG)
+            for name, quarter in quarters_due(step):
+                group_weight(name, quarter, 1)
+
+            for j, g in diff_groups_due(step):
                 weigh_diff(j, g)
-            quantizes(step)
-            for j, g in diff_parts(step):
-                quantize_a(j, g)
-            products(step)
+            for name, quarter in quarters_due(step - 1):
+                quantize_weight(name, quarter)
+            when_due(quantize_y, y_unit - QUANTIZE_LAG["y"])
+            when_due(lambda unit: quantize_rows("u", unit), u_unit - QUANTIZE_LAG["u"])
+            when_due(lambda unit: quantize_rows("t", unit), t_unit - QUANTIZE_LAG["t"])
+            when_due(round_y_on_vector, y_unit - SUM_LAG)
+            for j, g in diff_groups_due(step):
+                if g == 0:
+                    quantize_a(j, 0, 1)
+                elif g == SNP_GROUPS - 1:
+                    quantize_a(j, 1, SNP_GROUPS)
+
+            when_due(lambda unit: multiply("t", unit, "a", e_operand, SNP_GROUPS), t_unit)
+            when_due(lambda unit: multiply("u", unit, "t", weight_operand("mix"), GROUPS), u_unit)
+            when_due(lambda unit: multiply("y", unit, "u", weight_operand("combo"), GROUPS), y_unit)

from contextlib import ExitStack

import concourse.mybir as mybir
from concourse.masks import make_identity

F32 = mybir.dt.float32
BF16 = mybir.dt.bfloat16
I32 = mybir.dt.int32
U32 = mybir.dt.uint32
U8 = mybir.dt.uint8
FP8X4 = mybir.dt.float8_e4m3fn_x4
FP4X4 = mybir.dt.float4_e2m1fn_x4
ALU = mybir.AluOpType

ROWS, SNPS, RIGHT, COMBOS = 1280, 1536, 1024, 1024
FLOPS = 2 * ROWS * (SNPS * RIGHT + RIGHT * RIGHT + RIGHT * COMBOS)

P = 128
GROUP = 512
BAND = 2 * P
HALF = GROUP // 2
BANDS = ROWS // BAND
SNP_GROUPS = SNPS // GROUP
GROUPS = RIGHT // GROUP
UNITS = BANDS * GROUPS
QUARTERS = GROUPS * GROUPS
QUADRANTS = 4
BANKS = 8

SUM_LAG = 1
TURN_LAG = {"t": 3, "u": 2, "y": 3}
QUANTIZE_LAG = {"t": 3, "u": 3, "y": 4}
T_STEP = 1
U_STEP = T_STEP + GROUPS + QUANTIZE_LAG["t"]
Y_STEP = U_STEP + GROUPS + QUANTIZE_LAG["u"]
MIX_STEP, COMBO_STEP = U_STEP - QUARTERS, Y_STEP - QUARTERS
LAST_BAND_UNIT = UNITS - GROUPS
EARLY_BANDS = 3


def tile_f4_table_update_k1_kernel(
    tc, diff, snp_weight, e_words, e_scales, table, mix, combo, left_scale, offset, out_0, out_1, out_2
):
    nc = tc.nc
    with ExitStack() as ctx:
        keep = ctx.enter_context(tc.tile_pool(name="keep", bufs=1))
        work = ctx.enter_context(tc.tile_pool(name="work", bufs=1))
        psum = ctx.enter_context(tc.psum_pool(name="psum", bufs=1))
        ctx.enter_context(tc.manual_schedule())

        banks_taken = []

        def new_bank():
            name = "bank%d" % (len(banks_taken) % BANKS)
            banks_taken.append(name)
            return psum.tile([P, GROUP], F32, name=name)

        def band_rows(matrix, j):
            return matrix[BAND * j : BAND * (j + 1), :].rearrange("(p h) c -> p h c", h=2)

        def group_span(g):
            return slice(GROUP * g, GROUP * (g + 1))

        def read_sorted(ap):
            return ap.rearrange("p (m u e) -> p u m e", u=2, e=2)

        def lies_sorted(ap):
            return ap.rearrange("p (u m e) -> p u m e", u=2, e=2)

        def flat(ap):
            return ap.rearrange("p a b -> p (a b)")

        ident = keep.tile([P, P], F32, name="ident")
        make_identity(nc, ident[:])
        e_scale_sb = keep.tile([P, SNP_GROUPS, RIGHT], U8, name="e_scale_sb", align_bytes=64)
        nc.vector.memset(e_scale_sb[:].bitcast(I32), 0)

        diff_twins, table_sb, e_codes, weight_rows = {}, {}, {}, {}

        def load_diff(j):
            band = work.tile([P, 2, SNPS], BF16, name="diff_band", tag="rows", bufs=4)
            nc.sync.dma_start(out=band[:], in_=band_rows(diff, j))
            for g in range(SNP_GROUPS):
                diff_twins[j, g] = band[:, :, group_span(g)].bitcast(F32)

        def load_first_diff(g):
            part = keep.tile([P, 2, GROUP], BF16, name="diff_first%d" % g)
            nc.sync.dma_start(out=part[:], in_=band_rows(diff, 0)[:, :, group_span(g)])
            diff_twins[0, g] = part[:].bitcast(F32)

        def load_table(j):
            table_sb[j] = keep.tile([P, 2, RIGHT], BF16, name="table%d" % j)
            nc.sync.dma_start(out=table_sb[j][:], in_=band_rows(table, j))

        def load_e_codes(n):
            e_codes[n] = keep.tile([P, SNP_GROUPS, 2 * GROUP], U8, name="e_codes%d" % n, align_bytes=64)
            source = e_words.rearrange("g p b -> p g b")[:, :, 2 * GROUP * n : 2 * GROUP * (n + 1)]
            nc.sync.dma_start(out=e_codes[n][:].bitcast(I32), in_=source.bitcast(I32))

        def load_quarter(name, matrix, quarter):
            n, g = divmod(quarter, GROUPS)
            rows = keep.tile([P, 4, GROUP], BF16, name="%s_rows%d" % (name, quarter))
            nc.sync.dma_start(out=rows[:], in_=matrix[group_span(g), group_span(n)].rearrange("(p t) c -> p t c", t=4))
            weight_rows[name, quarter] = rows

        snp_weight_sb = keep.tile([P, SNP_GROUPS, 4], BF16, name="snp_weight_sb")
        nc.sync.dma_start(out=snp_weight_sb[:], in_=snp_weight.rearrange("(g p t) -> p g t", p=P, t=4))
        for g in range(SNP_GROUPS):
            load_first_diff(g)
        for q in range(QUADRANTS):
            nc.sync.dma_start(
                out=e_scale_sb[32 * q : 32 * q + 4].bitcast(I32),
                in_=e_scales[:, 4 * q : 4 * q + 4, :].rearrange("g r n -> r g n").bitcast(I32),
            )
        load_e_codes(0)
        load_diff(1)
        load_table(0)
        load_e_codes(1)
        row_loads = []
        for j in range(1, BANDS):
            if j + 1 < BANDS:
                row_loads.append((load_diff, j + 1))
            row_loads.append((load_table, j))
        quarter_loads = [
            (name, matrix, quarter) for name, matrix in (("mix", mix), ("combo", combo)) for quarter in range(QUARTERS)
        ]
        for i, (name, matrix, quarter) in enumerate(quarter_loads):
            load_quarter(name, matrix, quarter)
            if i < len(row_loads):
                load_rows, j = row_loads[i]
                load_rows(j)
        left_scale_sb = keep.tile([P, BANDS, 2], BF16, name="left_scale_sb")
        nc.sync.dma_start(out=left_scale_sb[:], in_=left_scale.rearrange("(j p h) -> p j h", p=P, h=2))
        offset_sb = keep.tile([P, COMBOS], BF16, name="offset_sb")
        nc.sync.dma_start(out=offset_sb[:], in_=offset.partition_broadcast(P))

        def mx_tiles(pool, name, groups, width, bufs):
            codes = pool.tile([P, groups, width], U32, name=name + "_codes", bufs=bufs, align_bytes=64)
            scales = pool.tile([P, groups, width], U8, name=name + "_scales", bufs=bufs, align_bytes=64)
            return codes, scales

        def quantize(codes, scales, grouped):
            nc.vector.quantize_mx(out=flat(codes).bitcast(FP8X4), scales=flat(scales), in_=flat(grouped))

        def new_grouped(name, parts, bufs):
            return work.tile([P, parts, 4 * BAND], BF16, name=name, bufs=bufs, align_bytes=64)

        def new_rounded():
            return work.tile([P, 2, GROUP], BF16, name="rounded", bufs=6)

        weight_mx = {name: mx_tiles(keep, name, GROUPS, RIGHT, 1) for name in ("mix", "combo")}
        y_codes = [keep.tile([P, GROUPS, BAND], U32, name="y_codes%d" % j, align_bytes=64) for j in range(BANDS)]
        y_scales = [
            keep.tile([P, GROUPS, BAND * EARLY_BANDS], U8, name="y_scales_early", align_bytes=64),
            keep.tile([P, GROUPS, BAND * (BANDS - EARLY_BANDS)], U8, name="y_scales_late", align_bytes=64),
        ]
        band_mx = {}
        held = {}

        def group_weight(name, quarter, half):
            if half == 0:
                held[name, quarter] = new_grouped("weight_grouped", 2, 3)
            nc.scalar.copy(
                out=held[name, quarter][:, half, :].rearrange("p (c i t) -> p c t i", i=4, t=4),
                in_=weight_rows[name, quarter][:, :, HALF * half : HALF * (half + 1)].rearrange("p t (c i) -> p c t i", i=4),
            )

        def quantize_weight(name, quarter):
            n, g = divmod(quarter, GROUPS)
            codes, scales = weight_mx[name]
            quantize(codes[:, g : g + 1, group_span(n)], scales[:, g : g + 1, group_span(n)], held.pop((name, quarter))[:])

        def turn_diff(j, g):
            bank = new_bank()
            outputs = bank[:].rearrange("p (u h r) -> p u h r", u=2, h=2)
            for h in range(2):
                for u in range(2):
                    nc.tensor.transpose(outputs[:, u, h, :], diff_twins[j, g][:, h, u::2], ident[:])
            held["a_bank", j, g] = bank

        def weigh_diff(j, g):
            if g == 0:
                held["a_grouped", j] = new_grouped("a_grouped", SNP_GROUPS, 2)
            nc.vector.tensor_tensor(
                out=held["a_grouped", j][:, g, :].rearrange("p (r u e) -> p r u e", u=2, e=2),
                in0=held.pop(("a_bank", j, g))[:].bitcast(BF16).rearrange("p (u r e) -> p r u e", u=2, e=2),
                in1=snp_weight_sb[:, g, :].rearrange("p (u e) -> p u e", e=2).unsqueeze(1).to_broadcast([P, BAND, 2, 2]),
                op=ALU.mult,
            )

        def quantize_a(j, first, last):
            if first == 0:
                band_mx["a", j] = mx_tiles(work, "a", SNP_GROUPS, BAND, 2)
            codes, scales = band_mx["a", j]
            quantize(codes[:, first:last, :], scales[:, first:last, :], held["a_grouped", j][:, first:last, :])

        def multiply(result, unit, stationary, moving, groups):
            j, n = divmod(unit, GROUPS)
            codes, scales = band_mx[stationary, j]
            for h in range(2):
                bank = new_bank()
                for g in range(groups):
                    rhs, rhs_scale = moving(g, n)
                    nc.tensor.matmul_mx(
                        out=bank[:],
                        lhsT=codes[:, g, P * h : P * (h + 1)].bitcast(FP8X4),
                        lhsT_scale=scales[:, g, P * h : P * (h + 1)],
                        rhs=rhs,
                        rhs_scale=rhs_scale,
                        start=(g == 0),
                        stop=(g == groups - 1),
                    )
                held[result, unit, h] = bank

        def e_operand(g, n):
            return e_codes[n][:, g, :].bitcast(FP4X4), e_scale_sb[:, g, group_span(n)]

        def weight_operand(name):
            codes, scales = weight_mx[name]
            return lambda g, n: (codes[:, g, group_span(n)].bitcast(FP8X4), scales[:, g, group_span(n)])

        def sum_t(unit):
            j, n = divmod(unit, GROUPS)
            t_f32 = work.tile([P, 2, GROUP], F32, name="t_f32", bufs=U_STEP - T_STEP + 2)
            rounded = new_rounded()
            for h in range(2):
                nc.vector.tensor_tensor(
                    out=lies_sorted(t_f32[:, h, :]),
                    in0=read_sorted(held.pop(("t", unit, h))[:]),
                    in1=read_sorted(table_sb[j][:, h, group_span(n)]),
                    op=ALU.add,
                )
                if gpsimd_rounds(unit, h):
                    nc.gpsimd.tensor_scalar(
                        out=rounded[:, h, :], in0=t_f32[:, h, :], scalar1=1.0, scalar2=0.0, op0=ALU.mult, op1=ALU.add
                    )
            held["t_f32", unit] = t_f32
            held["t_rounded", unit] = rounded

        def gpsimd_rounds(unit, h):
            step = T_STEP + unit + SUM_LAG
            covered = h == 0 or step > U_STEP or len(diff_groups_due(step)) > 1
            return unit < LAST_BAND_UNIT and covered

        def round_t_on_scalar(unit):
            for h in range(2):
                if not gpsimd_rounds(unit, h):
                    nc.scalar.copy(out=held["t_rounded", unit][:, h, :], in_=held["t_f32", unit][:, h, :])

        def sum_u(unit):
            t_f32 = held.pop(("t_f32", unit))
            rounded = new_rounded()
            for h in range(2):
                nc.vector.tensor_tensor(
                    out=lies_sorted(rounded[:, h, :]),
                    in0=read_sorted(held.pop(("u", unit, h))[:]),
                    in1=lies_sorted(t_f32[:, h, :]),
                    op=ALU.add,
                )
            held["u_rounded", unit] = rounded

        def sum_y(unit):
            j, n = divmod(unit, GROUPS)
            y_f32 = work.tile([P, 2, GROUP], F32, name="y_f32", tag="rows", bufs=4)
            for h in range(2):
                nc.vector.scalar_tensor_tensor(
                    out=y_f32[:, h, :],
                    in0=held.pop(("y", unit, h))[:],
                    scalar=left_scale_sb[:, j, h : h + 1],
                    in1=offset_sb[:, group_span(n)],
                    op0=ALU.mult,
                    op1=ALU.add,
                )
            nc.sync.dma_start(out=band_rows(out_0, j)[:, :, group_span(n)], in_=y_f32[:])
            held["y_f32", unit] = y_f32

        def round_y(copy, unit, h):
            copy(out=lies_sorted(held["y_rounded", unit][:, h, :]), in_=read_sorted(held["y_f32", unit][:, h, :]))

        def round_y_on_scalar(unit):
            held["y_rounded", unit] = new_rounded()
            round_y(nc.scalar.copy, unit, 0)
            if unit < LAST_BAND_UNIT:
                round_y(nc.scalar.copy, unit, 1)

        def round_y_on_vector(unit):
            if unit >= LAST_BAND_UNIT:
                round_y(nc.vector.tensor_copy, unit, 1)

        def turn(name, unit):
            twins = held.pop((name + "_rounded", unit))[:].bitcast(F32)
            bank = new_bank()
            outputs = bank[:].rearrange("p (u h r) -> p u h r", u=2, h=2)
            for h in range(2):
                for u in range(2):
                    nc.tensor.transpose(outputs[:, u, h, :], twins[:, h, P * u : P * (u + 1)], ident[:])
            held[name + "_bank", unit] = bank

        def group_rows(name, unit):
            j, n = divmod(unit, GROUPS)
            if n == 0:
                held[name + "_grouped", j] = new_grouped(name + "_grouped", GROUPS, 2)
            nc.scalar.copy(
                out=held[name + "_grouped", j][:, n, :].bitcast(F32).rearrange("p (r u) -> p r u", u=2),
                in_=held.pop((name + "_bank", unit))[:].rearrange("p (u r) -> p r u", u=2),
            )

        def group_y(unit):
            grouped = new_grouped("y_grouped", 1, 3)
            nc.scalar.copy(
                out=grouped[:, 0, :].bitcast(F32).rearrange("p (r h u) -> p r h u", h=2, u=2),
                in_=held.pop(("y_bank", unit))[:].rearrange("p (u h r) -> p r h u", u=2, h=2),
            )
            held["y_grouped", unit] = grouped

        def quantize_rows(name, unit):
            j, n = divmod(unit, GROUPS)
            if n == GROUPS - 1:
                band_mx[name, j] = mx_tiles(work, name, GROUPS, BAND, 3)
                codes, scales = band_mx[name, j]
                quantize(codes[:], scales[:], held.pop((name + "_grouped", j))[:])

        def store_y_codes(j, first, last):
            nc.sync.dma_start(
                out=out_1[first:last, :, BAND * j : BAND * (j + 1), :].rearrange("g p m t -> p g (m t)").bitcast(I32),
                in_=y_codes[j][:, first:last, :].bitcast(I32),
            )

        def quantize_y(unit):
            j, n = divmod(unit, GROUPS)
            late = j >= EARLY_BANDS
            first, last = (EARLY_BANDS, BANDS) if late else (0, EARLY_BANDS)
            scales = y_scales[late]
            quantize(
                y_codes[j][:, n : n + 1, :],
                scales[:, n : n + 1, BAND * (j - first) : BAND * (j - first + 1)],
                held.pop(("y_grouped", unit))[:],
            )
            if j == BANDS - 1:
                store_y_codes(j, n, n + 1)
            elif n == GROUPS - 1:
                store_y_codes(j, 0, GROUPS)
            if n == GROUPS - 1 and j + 1 == last:
                rows = slice(BAND * first, BAND * last)
                for q in range(QUADRANTS):
                    nc.sync.dma_start(
                        out=out_2[:, 4 * q : 4 * q + 4, rows].rearrange("g r m -> r g m").bitcast(I32),
                        in_=scales[32 * q : 32 * q + 4].bitcast(I32),
                    )

        def when_due(action, unit):
            if 0 <= unit < UNITS:
                action(unit)

        def quarters_due(step):
            starts = (("mix", MIX_STEP), ("combo", COMBO_STEP))
            return [(name, step - first) for name, first in starts if 0 <= step - first < QUARTERS]

        def diff_groups_due(step):
            j, early = (step + 1) // 2, step % 2 == 1
            if not 1 <= j < BANDS:
                return []
            if j == 1:
                return [] if early else [(j, 0), (j, 1), (j, 2)]
            return [(j, 0)] if early else [(j, 1), (j, 2)]

        for g in range(SNP_GROUPS):
            turn_diff(0, g)
            weigh_diff(0, g)
            if g > 0:
                quantize_a(0, g - 1, g)
        quantize_a(0, SNP_GROUPS - 1, SNP_GROUPS)

        for step in range(T_STEP, Y_STEP + UNITS + QUANTIZE_LAG["y"]):
            t_unit, u_unit, y_unit = step - T_STEP, step - U_STEP, step - Y_STEP

            when_due(sum_t, t_unit - SUM_LAG)
            when_due(sum_u, u_unit - SUM_LAG)
            when_due(sum_y, y_unit - SUM_LAG)

            when_due(lambda unit: turn("y", unit), y_unit - TURN_LAG["y"])
            when_due(lambda unit: turn("u", unit), u_unit - TURN_LAG["u"])
            when_due(lambda unit: turn("t", unit), t_unit - TURN_LAG["t"])
            for j, g in diff_groups_due(step):
                turn_diff(j, g)

            round_y_first = y_unit - SUM_LAG >= LAST_BAND_UNIT
            for name, quarter in quarters_due(step):
                group_weight(name, quarter, 0)
            if round_y_first:
                when_due(round_y_on_scalar, y_unit - SUM_LAG)
            when_due(group_y, y_unit - TURN_LAG["y"])
            when_due(lambda unit: group_rows("u", unit), u_unit - TURN_LAG["u"])
            when_due(lambda unit: group_rows("t", unit), t_unit - TURN_LAG["t"])
            when_due(round_t_on_scalar, t_unit - SUM_LAG)
            if not round_y_first:
                when_due(round_y_on_scalar, y_unit - SUM_LAG)
            for name, quarter in quarters_due(step):
                group_weight(name, quarter, 1)

            for j, g in diff_groups_due(step):
                weigh_diff(j, g)
            for name, quarter in quarters_due(step - 1):
                quantize_weight(name, quarter)
            when_due(quantize_y, y_unit - QUANTIZE_LAG["y"])
            when_due(lambda unit: quantize_rows("u", unit), u_unit - QUANTIZE_LAG["u"])
            when_due(lambda unit: quantize_rows("t", unit), t_unit - QUANTIZE_LAG["t"])
            when_due(round_y_on_vector, y_unit - SUM_LAG)
            for j, g in diff_groups_due(step):
                if g == 0:
                    quantize_a(j, 0, 1)
                elif g == SNP_GROUPS - 1:
                    quantize_a(j, 1, SNP_GROUPS)

            when_due(lambda unit: multiply("t", unit, "a", e_operand, SNP_GROUPS), t_unit)
            when_due(lambda unit: multiply("u", unit, "t", weight_operand("mix"), GROUPS), u_unit)
            when_due(lambda unit: multiply("y", unit, "u", weight_operand("combo"), GROUPS), y_unit)
